import numpy as np
import ml_dtypes


def mxq(x, axis, fmt="e4m3"):
    dtype, down = {"e4m3": (ml_dtypes.float8_e4m3fn, 7), "e5m2": (ml_dtypes.float8_e5m2, 14)}[fmt]
    v = np.moveaxis(np.asarray(x, np.float32).astype(ml_dtypes.bfloat16).astype(np.float64), axis, -1)
    blocks = v.reshape(v.shape[:-1] + (-1, 32))
    amax = np.abs(blocks).max(-1, keepdims=True)
    byte = np.maximum(np.where(amax > 0, np.frexp(amax)[1] - 1 + 127, 0) - down, 1)
    scale = np.exp2(byte - 127.0)
    codes = (blocks / scale).astype(np.float32).astype(dtype).astype(np.float64)
    return np.moveaxis((codes * scale).reshape(v.shape), -1, axis)


WIDE = False


def mx_kscale(k):
    if not WIDE:
        return np.ones(k)
    levels = np.array([10, -10, 5, -5, 0])
    if k % 512:
        return np.exp2(np.random.permutation(np.resize(levels, k // 32))).repeat(32)
    a = np.empty((k // 512, 16))
    for p in range(k // 512):
        a[p, :8] = np.random.permutation(np.resize(levels, 8))
        for g in range(8):
            far = levels[np.abs(levels - a[p, g]) >= 10]
            a[p, g + 8] = far[np.random.randint(len(far))]
    return np.exp2(a.ravel()).repeat(32)


def f64(x):
    return np.asarray(x).astype(np.float64)


def striped(idx):
    return np.tile(np.asarray(idx).reshape(-1, 16).T, (8, 1)).astype(np.uint16)


def unstriped(offs):
    return offs[:16].T.reshape(-1).astype(np.int64)


E2M1 = np.array([0.0, 0.5, 1.0, 1.5, 2.0, 3.0, 4.0, 6.0, -0.0, -0.5, -1.0, -1.5, -2.0, -3.0, -4.0, -6.0])


def pack_weight(w, fmt):
    k, n = w.shape
    w = f64(np.asarray(w, np.float32).astype(ml_dtypes.bfloat16)).reshape(k // 32, 32, n)
    amax = np.abs(w).max(1)
    if fmt == "e4m3":
        byte = np.frexp(amax)[1] - 1 + 127 - 7
    else:
        mant, ex = np.frexp(amax / 6.0)
        byte = np.where(mant > 0.5, ex, ex - 1) + 127
    byte = np.clip(np.where(amax > 0, byte, 1), 1, 254)
    scaled = (w * np.exp2(127.0 - byte)[:, None, :]).reshape(k, n).astype(np.float32)
    by_word = np.ascontiguousarray(scaled.reshape(k // 512, 128, 4, n).transpose(0, 1, 3, 2))
    if fmt == "e4m3":
        words = by_word.astype(ml_dtypes.float8_e4m3fn).view(np.uint8)
    else:
        c = by_word.astype(ml_dtypes.float4_e2m1fn).view(np.uint8) & 0xF
        words = (c[..., 0::2] | (c[..., 1::2] << 4)).reshape(k // 512, 128, 2 * n)
    return np.ascontiguousarray(words), np.ascontiguousarray(byte.astype(np.uint8).reshape(k // 512, 16, n))


def unpack_weight(words, scales, fmt):
    g, _, n = scales.shape
    words = np.ascontiguousarray(words).reshape(g, 128, n, -1)
    if fmt == "e4m3":
        vals = words.view(ml_dtypes.float8_e4m3fn).astype(np.float64)
    else:
        nib = np.empty((g, 128, n, 4), np.uint8)
        nib[..., 0::2] = words & 0xF
        nib[..., 1::2] = words >> 4
        vals = E2M1[nib]
    vals = vals * np.repeat(np.exp2(scales.astype(np.float64) - 127.0), 8, axis=1)[..., None]
    return vals.transpose(0, 1, 3, 2).reshape(g * 512, n)


def bf(x):
    return np.asarray(x, np.float32).astype(ml_dtypes.bfloat16)


def planes(Y):
    r, m = Y.shape
    b = f64(bf(Y)).reshape(r // 32, 32, m)
    amax = np.abs(b).max(1)
    byte = np.clip(np.where(amax > 0, np.frexp(amax)[1] - 1 + 127 - 7, 1), 1, 254)
    codes = (b * np.exp2(127.0 - byte)[:, None, :]).reshape(r, m).astype(np.float32).astype(ml_dtypes.float8_e4m3fn).view(np.uint8)
    words = codes.reshape(r // 512, 128, 4, m).transpose(0, 1, 3, 2)
    return np.ascontiguousarray(words), np.ascontiguousarray(byte.astype(np.uint8).reshape(r // 512, 16, m))


D, K, T, I, U, Q = 512, 512, 2048, 512, 256, 256


def setup_inputs():
    n = np.random.standard_normal
    idx = np.random.permutation(T)[:I]
    idx2 = np.random.randint(0, U, I)
    fd = mx_kscale(D)
    pkptp = pack_weight(n((D, T)) / fd[:, None], "e2m1")
    return {
        "pts": (n((D, T)) / fd[:, None]).astype(np.float32),
        "mean": (n((D, U)) * 0.7 / fd[:, None]).astype(np.float32),
        "white": (n((D, K)) * 1 / np.sqrt(D) * fd[:, None]).astype(np.float32),
        "pkpt_words": pkptp[0],
        "pkpt_scales": pkptp[1],
        "query": (n((D, Q)) * 1 / np.sqrt(D) * fd[:, None]).astype(np.float32),
        "sharp": (np.random.uniform(0.5, 2.0, (I, 1))).astype(np.float32),
        "offs": striped(idx),
        "offs2": striped(idx2),
    }


def reference(pts, mean, white, pkpt_words, pkpt_scales, query, sharp, offs, offs2):
    idx = unstriped(offs)
    idx2 = unstriped(offs2)
    pkptu = unpack_weight(pkpt_words, pkpt_scales, "e2m1")
    xc = f64(pts)[:, idx] - f64(mean)[:, idx2]
    xcq = mxq(xc, 0, "e4m3")
    whiteq = mxq(f64(white), 0, "e4m3")
    z = xcq.T @ whiteq
    en = np.mean(np.square(z), axis=1, keepdims=True) * f64(sharp)
    pkptidxg = pkptu[:, idx]
    queryq = mxq(f64(query), 0, "e4m3")
    a = pkptidxg.T @ queryq
    y = a - en
    words, scales = planes(y)
    return y, words, scales

@@ -1,0 +1,148 @@
+from contextlib import ExitStack
+
+import concourse.mybir as mybir
+
+D, K, T, I, U, Q = 512, 512, 2048, 512, 256, 256
+FLOPS = 2 * D * I * (K + Q)
+
+F32 = mybir.dt.float32
+BF16 = mybir.dt.bfloat16
+I32 = mybir.dt.int32
+U32 = mybir.dt.uint32
+U16 = mybir.dt.uint16
+U8 = mybir.dt.uint8
+FP8X4 = mybir.dt.float8_e4m3fn_x4
+FP4X4 = mybir.dt.float4_e2m1fn_x4
+ALU = mybir.AluOpType
+ACT = mybir.ActivationFunctionType
+
+P = 128
+PACK = 4
+MEAN_WINDOW = 704
+VECTOR_ROWS = 80
+
+
+def tile_attend_energyscores_pl_kernel(tc, pts, mean, white, pkpt_words, pkpt_scales, query, sharp, offs, offs2,
+                                        out_0, out_1, out_2):
+    nc = tc.nc
+    with ExitStack() as ctx:
+        sb = ctx.enter_context(tc.tile_pool(name="sb", bufs=1))
+        psum = ctx.enter_context(tc.psum_pool(name="psum", bufs=1))
+
+        offsets = sb.tile([P, I // 16], U16, name="offsets")
+        offsets2 = sb.tile([P, I // 16], U16, name="offsets2")
+        key_scales = sb.tile([P, T], U8, name="key_scales", align_bytes=64)
+        key_words = sb.tile([P, T], U16, name="key_words", align_bytes=64)
+        mean_first = sb.tile([P, MEAN_WINDOW], F32, name="mean_first")
+        mean_rest = sb.tile([P, 2 * U + MEAN_WINDOW], F32, name="mean_rest")
+        pts_planes = [sb.tile([P, T], F32, name=f"pts_plane{t}") for t in range(PACK)]
+        white_raw = sb.tile([P, PACK, K], F32, name="white_raw")
+        query_raw = sb.tile([P, PACK, Q], F32, name="query_raw")
+        sharp_cols = sb.tile([P, PACK], F32, name="sharp_cols")
+
+        nc.vector.memset(key_scales[:].bitcast(I32), 0)
+        nc.vector.memset(mean_first[:, U:], 0.0)
+        nc.vector.memset(mean_rest[:, 3 * U:], 0.0)
+
+        mean_rows = mean.rearrange("(p t) u -> p (t u)", t=PACK)
+        pts_rows = pts.rearrange("(p t) c -> t p c", t=PACK)
+        nc.sync.dma_start(offsets2[:], offs2)
+        nc.sync.dma_start(mean_first[:, :U], mean_rows[:, :U])
+        nc.sync.dma_start(mean_rest[:, :3 * U], mean_rows[:, U:])
+        nc.sync.dma_start(offsets[:], offs)
+        for quad in range(4):
+            nc.scalar.dma_start(key_scales[32 * quad:32 * quad + 4, :].bitcast(I32),
+                                pkpt_scales[0, 4 * quad:4 * quad + 4, :].bitcast(I32))
+        nc.scalar.dma_start(sharp_cols[:], sharp.rearrange("(p r) o -> p (r o)", r=PACK))
+        nc.sync.dma_start(pts_planes[0][:], pts_rows[0])
+        nc.sync.dma_start(white_raw[:], white.rearrange("(p t) k -> p t k", t=PACK))
+        for t in range(1, PACK):
+            nc.sync.dma_start(pts_planes[t][:], pts_rows[t])
+        nc.sync.dma_start(key_words[:].bitcast(I32), pkpt_words[0].bitcast(I32))
+        nc.sync.dma_start(query_raw[:], query.rearrange("(p t) q -> p t q", t=PACK))
+
+        neg_sharp = sb.tile([P, PACK], F32, name="neg_sharp")
+        nc.scalar.activation(neg_sharp[:], sharp_cols[:], ACT.Copy, scale=-1.0 / K)
+
+        mean_g = [sb.tile([P, I], F32, name=f"mean_g{t}") for t in range(PACK)]
+        nc.vector.tensor_copy(mean_g[0][:], mean_first[:].indirect(offsets2[:]))
+        for t in range(1, PACK):
+            start = (t - 1) * U
+            nc.vector.tensor_copy(mean_g[t][:], mean_rest[:, start:start + MEAN_WINDOW].indirect(offsets2[:]))
+
+        scales_g = sb.tile([P, I], U8, name="scales_g", align_bytes=64)
+        scales_d = sb.tile([P, PACK, P], U8, name="scales_d", align_bytes=64)
+        nc.vector.tensor_copy(scales_g[:], key_scales[:].indirect(offsets[:]))
+
+        white_il = sb.tile([P, K * PACK], BF16, name="white_il", align_bytes=64)
+        nc.scalar.copy(white_il[:].rearrange("p (c i t) -> p c t i", i=4, t=PACK),
+                       white_raw[:].rearrange("p t (c i) -> p c t i", i=4))
+        white_codes = sb.tile([P, K], U32, name="white_codes", align_bytes=64)
+        white_scales = sb.tile([P, K], U8, name="white_scales", align_bytes=64)
+
+        xc = sb.tile([P, PACK, I], F32, name="xc")
+        for t in range(PACK):
+            nc.vector.tensor_tensor(xc[:, t, :], pts_planes[t][:].indirect(offsets[:]), mean_g[t][:], ALU.subtract)
+            if t == 0:
+                nc.vector.tensor_copy(scales_d[:], scales_g[:].rearrange("p (s r) -> p r s", r=PACK))
+            if t == 1:
+                nc.vector.quantize_mx(white_codes[:].bitcast(FP8X4), white_scales[:], white_il[:])
+
+        xc_il = sb.tile([P, I * PACK], BF16, name="xc_il", align_bytes=64)
+        dealt_out = xc_il[:].rearrange("p (r s t) -> p s t r", r=PACK, t=PACK)
+        dealt_in = xc[:].rearrange("p t (s r) -> p s t r", r=PACK)
+        nc.vector.tensor_copy(dealt_out[:, :VECTOR_ROWS], dealt_in[:, :VECTOR_ROWS])
+        nc.scalar.copy(dealt_out[:, VECTOR_ROWS:], dealt_in[:, VECTOR_ROWS:])
+
+        xc_codes = [sb.tile([P, 2 * P], U32, name=f"xc_codes{h}", align_bytes=64) for h in range(2)]
+        xc_scales = [sb.tile([P, 2 * P], U8, name=f"xc_scales{h}", align_bytes=64) for h in range(2)]
+        for h in range(2):
+            nc.vector.quantize_mx(xc_codes[h][:].bitcast(FP8X4), xc_scales[h][:],
+                                  xc_il[:, h * 2 * I:(h + 1) * 2 * I])
+
+        query_il = sb.tile([P, Q * PACK], BF16, name="query_il", align_bytes=64)
+        nc.scalar.copy(query_il[:].rearrange("p (c i t) -> p c t i", i=4, t=PACK),
+                       query_raw[:].rearrange("p t (c i) -> p c t i", i=4))
+
+        sums = sb.tile([P, PACK], F32, name="sums")
+        squares = sb.tile([P, K], BF16, name="squares")
+        for r in range(PACK):
+            z = psum.tile([P, K], F32, name=f"z{r}")
+            cols = slice((r % 2) * P, (r % 2 + 1) * P)
+            nc.tensor.matmul_mx(z[:], lhsT=xc_codes[r // 2][:, cols].bitcast(FP8X4),
+                                lhsT_scale=xc_scales[r // 2][:, cols],
+                                rhs=white_codes[:].bitcast(FP8X4), rhs_scale=white_scales[:],
+                                start=True, stop=True)
+            nc.scalar.activation(squares[:], z[:], ACT.Square, accum_out=sums[:, r:r + 1])
+
+        words_g = sb.tile([P, I], U16, name="words_g", align_bytes=64)
+        words_d = sb.tile([P, PACK, P], U16, name="words_d", align_bytes=64)
+        query_codes = sb.tile([P, Q], U32, name="query_codes", align_bytes=64)
+        query_scales = sb.tile([P, Q], U8, name="query_scales", align_bytes=64)
+        nc.vector.tensor_copy(words_g[:], key_words[:].indirect(offsets[:]))
+        nc.vector.quantize_mx(query_codes[:].bitcast(FP8X4), query_scales[:], query_il[:])
+        nc.vector.tensor_copy(words_d[:], words_g[:].rearrange("p (s r) -> p r s", r=PACK))
+
+        y = sb.tile([P, PACK, Q], F32, name="y")
+        out_rows = out_0.rearrange("(p r) q -> p r q", r=PACK)
+        for r in range(PACK):
+            a = psum.tile([P, Q], F32, name=f"a{r}")
+            nc.tensor.matmul_mx(a[:], lhsT=words_d[:, r, :].bitcast(FP4X4), lhsT_scale=scales_d[:, r, :],
+                                rhs=query_codes[:].bitcast(FP8X4), rhs_scale=query_scales[:],
+                                start=True, stop=True)
+            nc.vector.scalar_tensor_tensor(y[:, r, :], neg_sharp[:, r:r + 1].to_broadcast([P, Q]),
+                                           sums[:, r:r + 1], a[:], ALU.mult, ALU.add)
+            if r % 2 == 1:
+                nc.sync.dma_start(out_rows[:, r - 1:r + 1, :], y[:, r - 1:r + 1, :])
+
+        y_il = sb.tile([P, Q * PACK], BF16, name="y_il", align_bytes=64)
+        y_codes = sb.tile([P, Q], U32, name="y_codes", align_bytes=64)
+        y_scales = sb.tile([P, Q], U8, name="y_scales", align_bytes=64)
+        nc.vector.tensor_copy(y_il[:].rearrange("p (c i r) -> p c r i", i=4, r=PACK),
+                              y[:].rearrange("p r (c i) -> p c r i", i=4))
+        nc.vector.quantize_mx(y_codes[:].bitcast(FP8X4), y_scales[:], y_il[:])
+        nc.sync.dma_start(out_1[0].rearrange("p c r -> p (c r)").bitcast(I32), y_codes[:].bitcast(I32))
+        for quad in range(4):
+            queue = nc.scalar if quad % 2 == 0 else nc.sync
+            queue.dma_start(out_2[0, 4 * quad:4 * quad + 4, :].bitcast(I32),
+                            y_scales[32 * quad:32 * quad + 4, :].bitcast(I32))

@@ -19,7 +19,7 @@ ACT = mybir.ActivationFunctionType
 P = 128
 PACK = 4
 MEAN_WINDOW = 704
-VECTOR_ROWS = 80
+VECTOR_RUNS = 44
 
 
 def tile_attend_energyscores_pl_kernel(tc, pts, mean, white, pkpt_words, pkpt_scales, query, sharp, offs, offs2,
@@ -36,7 +36,7 @@ def tile_attend_energyscores_pl_kernel(tc, pts, mean, white, pkpt_words, pkpt_sc
         mean_first = sb.tile([P, MEAN_WINDOW], F32, name="mean_first")
         mean_rest = sb.tile([P, 2 * U + MEAN_WINDOW], F32, name="mean_rest")
         pts_planes = [sb.tile([P, T], F32, name=f"pts_plane{t}") for t in range(PACK)]
-        white_raw = sb.tile([P, PACK, K], F32, name="white_raw")
+        white_raw = [sb.tile([P, PACK, K // 2], F32, name=f"white_raw{h}") for h in range(2)]
         query_raw = sb.tile([P, PACK, Q], F32, name="query_raw")
         sharp_cols = sb.tile([P, PACK], F32, name="sharp_cols")
 
@@ -46,63 +46,72 @@ def tile_attend_energyscores_pl_kernel(tc, pts, mean, white, pkpt_words, pkpt_sc
 
         mean_rows = mean.rearrange("(p t) u -> p (t u)", t=PACK)
         pts_rows = pts.rearrange("(p t) c -> t p c", t=PACK)
+        white_rows = white.rearrange("(p t) (h k) -> h p t k", t=PACK, h=2)
         nc.sync.dma_start(offsets2[:], offs2)
         nc.sync.dma_start(mean_first[:, :U], mean_rows[:, :U])
         nc.sync.dma_start(mean_rest[:, :3 * U], mean_rows[:, U:])
         nc.sync.dma_start(offsets[:], offs)
-        for quad in range(4):
-            nc.scalar.dma_start(key_scales[32 * quad:32 * quad + 4, :].bitcast(I32),
-                                pkpt_scales[0, 4 * quad:4 * quad + 4, :].bitcast(I32))
-        nc.scalar.dma_start(sharp_cols[:], sharp.rearrange("(p r) o -> p (r o)", r=PACK))
         nc.sync.dma_start(pts_planes[0][:], pts_rows[0])
-        nc.sync.dma_start(white_raw[:], white.rearrange("(p t) k -> p t k", t=PACK))
+        for quad in range(4):
+            nc.sync.dma_start(key_scales[32 * quad:32 * quad + 4, :].bitcast(I32),
+                              pkpt_scales[0, 4 * quad:4 * quad + 4, :].bitcast(I32))
+        nc.sync.dma_start(sharp_cols[:], sharp.rearrange("(p r) o -> p (r o)", r=PACK))
         for t in range(1, PACK):
             nc.sync.dma_start(pts_planes[t][:], pts_rows[t])
-        nc.sync.dma_start(key_words[:].bitcast(I32), pkpt_words[0].bitcast(I32))
+        for h in range(2):
+            nc.sync.dma_start(white_raw[h][:], white_rows[h])
         nc.sync.dma_start(query_raw[:], query.rearrange("(p t) q -> p t q", t=PACK))
+        nc.sync.dma_start(key_words[:].bitcast(I32), pkpt_words[0].bitcast(I32))
 
         neg_sharp = sb.tile([P, PACK], F32, name="neg_sharp")
         nc.scalar.activation(neg_sharp[:], sharp_cols[:], ACT.Copy, scale=-1.0 / K)
 
-        mean_g = [sb.tile([P, I], F32, name=f"mean_g{t}") for t in range(PACK)]
-        nc.vector.tensor_copy(mean_g[0][:], mean_first[:].indirect(offsets2[:]))
+        mean_g = sb.tile([P, PACK, I], F32, name="mean_g")
+        pts_g = sb.tile([P, PACK, I], F32, name="pts_g")
+        nc.vector.tensor_copy(mean_g[:, 0, :], mean_first[:].indirect(offsets2[:]))
         for t in range(1, PACK):
             start = (t - 1) * U
-            nc.vector.tensor_copy(mean_g[t][:], mean_rest[:, start:start + MEAN_WINDOW].indirect(offsets2[:]))
-
+            nc.vector.tensor_copy(mean_g[:, t, :], mean_rest[:, start:start + MEAN_WINDOW].indirect(offsets2[:]))
         scales_g = sb.tile([P, I], U8, name="scales_g", align_bytes=64)
         scales_d = sb.tile([P, PACK, P], U8, name="scales_d", align_bytes=64)
         nc.vector.tensor_copy(scales_g[:], key_scales[:].indirect(offsets[:]))
-
-        white_il = sb.tile([P, K * PACK], BF16, name="white_il", align_bytes=64)
-        nc.scalar.copy(white_il[:].rearrange("p (c i t) -> p c t i", i=4, t=PACK),
-                       white_raw[:].rearrange("p t (c i) -> p c t i", i=4))
-        white_codes = sb.tile([P, K], U32, name="white_codes", align_bytes=64)
-        white_scales = sb.tile([P, K], U8, name="white_scales", align_bytes=64)
-
-        xc = sb.tile([P, PACK, I], F32, name="xc")
         for t in range(PACK):
-            nc.vector.tensor_tensor(xc[:, t, :], pts_planes[t][:].indirect(offsets[:]), mean_g[t][:], ALU.subtract)
+            nc.vector.tensor_copy(pts_g[:, t, :], pts_planes[t][:].indirect(offsets[:]))
             if t == 0:
                 nc.vector.tensor_copy(scales_d[:], scales_g[:].rearrange("p (s r) -> p r s", r=PACK))
-            if t == 1:
-                nc.vector.quantize_mx(white_codes[:].bitcast(FP8X4), white_scales[:], white_il[:])
 
-        xc_il = sb.tile([P, I * PACK], BF16, name="xc_il", align_bytes=64)
-        dealt_out = xc_il[:].rearrange("p (r s t) -> p s t r", r=PACK, t=PACK)
-        dealt_in = xc[:].rearrange("p t (s r) -> p s t r", r=PACK)
-        nc.vector.tensor_copy(dealt_out[:, :VECTOR_ROWS], dealt_in[:, :VECTOR_ROWS])
-        nc.scalar.copy(dealt_out[:, VECTOR_ROWS:], dealt_in[:, VECTOR_ROWS:])
-
+        xc_il = [sb.tile([P, 2 * I], BF16, name=f"xc_il{h}", align_bytes=64) for h in range(2)]
         xc_codes = [sb.tile([P, 2 * P], U32, name=f"xc_codes{h}", align_bytes=64) for h in range(2)]
         xc_scales = [sb.tile([P, 2 * P], U8, name=f"xc_scales{h}", align_bytes=64) for h in range(2)]
+        pts_dealt = pts_g[:].rearrange("p t (s r) -> p s t r", r=PACK)
+        mean_dealt = mean_g[:].rearrange("p t (s r) -> p s t r", r=PACK)
         for h in range(2):
-            nc.vector.quantize_mx(xc_codes[h][:].bitcast(FP8X4), xc_scales[h][:],
-                                  xc_il[:, h * 2 * I:(h + 1) * 2 * I])
+            nc.vector.tensor_tensor(xc_il[h][:].rearrange("p (r s t) -> p s t r", r=2, t=PACK),
+                                    pts_dealt[:, :, :, 2 * h:2 * h + 2], mean_dealt[:, :, :, 2 * h:2 * h + 2],
+                                    ALU.subtract)
+
+        white_codes = sb.tile([P, K], U32, name="white_codes", align_bytes=64)
+        white_scales = sb.tile([P, K], U8, name="white_scales", align_bytes=64)
+        for h in range(2):
+            white_il = sb.tile([P, K // 2 * PACK], BF16, name=f"white_il{h}", align_bytes=64)
+            nc.scalar.copy(white_il[:].rearrange("p (c i t) -> p c t i", i=4, t=PACK),
+                           white_raw[h][:].rearrange("p t (c i) -> p c t i", i=4))
+            cols = slice(h * K // 2, (h + 1) * K // 2)
+            nc.vector.quantize_mx(white_codes[:, cols].bitcast(FP8X4), white_scales[:, cols], white_il[:])
+        for h in range(2):
+            nc.vector.quantize_mx(xc_codes[h][:].bitcast(FP8X4), xc_scales[h][:], xc_il[h][:])
 
         query_il = sb.tile([P, Q * PACK], BF16, name="query_il", align_bytes=64)
         nc.scalar.copy(query_il[:].rearrange("p (c i t) -> p c t i", i=4, t=PACK),
                        query_raw[:].rearrange("p t (c i) -> p c t i", i=4))
+        query_codes = sb.tile([P, Q], U32, name="query_codes", align_bytes=64)
+        query_scales = sb.tile([P, Q], U8, name="query_scales", align_bytes=64)
+
+        words_g = sb.tile([P, I], U16, name="words_g", align_bytes=64)
+        words_d = sb.tile([P, PACK, P], U16, name="words_d", align_bytes=64)
+        nc.vector.tensor_copy(words_g[:], key_words[:].indirect(offsets[:]))
+        nc.vector.quantize_mx(query_codes[:].bitcast(FP8X4), query_scales[:], query_il[:])
+        nc.vector.tensor_copy(words_d[:], words_g[:].rearrange("p (s r) -> p r s", r=PACK))
 
         sums = sb.tile([P, PACK], F32, name="sums")
         squares = sb.tile([P, K], BF16, name="squares")
@@ -115,14 +124,6 @@ def tile_attend_energyscores_pl_kernel(tc, pts, mean, white, pkpt_words, pkpt_sc
                                 start=True, stop=True)
             nc.scalar.activation(squares[:], z[:], ACT.Square, accum_out=sums[:, r:r + 1])
 
-        words_g = sb.tile([P, I], U16, name="words_g", align_bytes=64)
-        words_d = sb.tile([P, PACK, P], U16, name="words_d", align_bytes=64)
-        query_codes = sb.tile([P, Q], U32, name="query_codes", align_bytes=64)
-        query_scales = sb.tile([P, Q], U8, name="query_scales", align_bytes=64)
-        nc.vector.tensor_copy(words_g[:], key_words[:].indirect(offsets[:]))
-        nc.vector.quantize_mx(query_codes[:].bitcast(FP8X4), query_scales[:], query_il[:])
-        nc.vector.tensor_copy(words_d[:], words_g[:].rearrange("p (s r) -> p r s", r=PACK))
-
         y = sb.tile([P, PACK, Q], F32, name="y")
         out_rows = out_0.rearrange("(p r) q -> p r q", r=PACK)
         for r in range(PACK):
@@ -130,16 +131,23 @@ def tile_attend_energyscores_pl_kernel(tc, pts, mean, white, pkpt_words, pkpt_sc
             nc.tensor.matmul_mx(a[:], lhsT=words_d[:, r, :].bitcast(FP4X4), lhsT_scale=scales_d[:, r, :],
                                 rhs=query_codes[:].bitcast(FP8X4), rhs_scale=query_scales[:],
                                 start=True, stop=True)
-            nc.vector.scalar_tensor_tensor(y[:, r, :], neg_sharp[:, r:r + 1].to_broadcast([P, Q]),
-                                           sums[:, r:r + 1], a[:], ALU.mult, ALU.add)
+            if r < PACK - 1:
+                nc.vector.scalar_tensor_tensor(y[:, r, :], neg_sharp[:, r:r + 1].to_broadcast([P, Q]),
+                                               sums[:, r:r + 1], a[:], ALU.mult, ALU.add)
+            else:
+                neg_energy = sb.tile([P, 1], F32, name=f"neg_energy{r}")
+                nc.scalar.activation(neg_energy[:], sums[:, r:r + 1], ACT.Copy, scale=neg_sharp[:, r:r + 1])
+                nc.scalar.activation(y[:, r, :], a[:], ACT.Identity, bias=neg_energy[:])
             if r % 2 == 1:
                 nc.sync.dma_start(out_rows[:, r - 1:r + 1, :], y[:, r - 1:r + 1, :])
 
         y_il = sb.tile([P, Q * PACK], BF16, name="y_il", align_bytes=64)
         y_codes = sb.tile([P, Q], U32, name="y_codes", align_bytes=64)
         y_scales = sb.tile([P, Q], U8, name="y_scales", align_bytes=64)
-        nc.vector.tensor_copy(y_il[:].rearrange("p (c i r) -> p c r i", i=4, r=PACK),
-                              y[:].rearrange("p r (c i) -> p c r i", i=4))
+        y_out = y_il[:].rearrange("p (c i r) -> p c r i", i=4, r=PACK)
+        y_in = y[:].rearrange("p r (c i) -> p c r i", i=4)
+        nc.vector.tensor_copy(y_out[:, :VECTOR_RUNS], y_in[:, :VECTOR_RUNS])
+        nc.scalar.copy(y_out[:, VECTOR_RUNS:], y_in[:, VECTOR_RUNS:])
         nc.vector.quantize_mx(y_codes[:].bitcast(FP8X4), y_scales[:], y_il[:])
         nc.sync.dma_start(out_1[0].rearrange("p c r -> p (c r)").bitcast(I32), y_codes[:].bitcast(I32))
         for quad in range(4):

@@ -52,9 +52,7 @@ def tile_attend_energyscores_pl_kernel(tc, pts, mean, white, pkpt_words, pkpt_sc
         nc.sync.dma_start(mean_rest[:, :3 * U], mean_rows[:, U:])
         nc.sync.dma_start(offsets[:], offs)
         nc.sync.dma_start(pts_planes[0][:], pts_rows[0])
-        for quad in range(4):
-            nc.sync.dma_start(key_scales[32 * quad:32 * quad + 4, :].bitcast(I32),
-                              pkpt_scales[0, 4 * quad:4 * quad + 4, :].bitcast(I32))
+        nc.sync.dma_start(key_scales[0:P:8, :].bitcast(I32), pkpt_scales[0].bitcast(I32))
         nc.sync.dma_start(sharp_cols[:], sharp.rearrange("(p r) o -> p (r o)", r=PACK))
         for t in range(1, PACK):
             nc.sync.dma_start(pts_planes[t][:], pts_rows[t])
@@ -67,7 +65,7 @@ def tile_attend_energyscores_pl_kernel(tc, pts, mean, white, pkpt_words, pkpt_sc
         nc.scalar.activation(neg_sharp[:], sharp_cols[:], ACT.Copy, scale=-1.0 / K)
 
         mean_g = sb.tile([P, PACK, I], F32, name="mean_g")
-        pts_g = sb.tile([P, PACK, I], F32, name="pts_g")
+        xc = sb.tile([P, PACK, I], F32, name="xc")
         nc.vector.tensor_copy(mean_g[:, 0, :], mean_first[:].indirect(offsets2[:]))
         for t in range(1, PACK):
             start = (t - 1) * U
@@ -76,19 +74,20 @@ def tile_attend_energyscores_pl_kernel(tc, pts, mean, white, pkpt_words, pkpt_sc
         scales_d = sb.tile([P, PACK, P], U8, name="scales_d", align_bytes=64)
         nc.vector.tensor_copy(scales_g[:], key_scales[:].indirect(offsets[:]))
         for t in range(PACK):
-            nc.vector.tensor_copy(pts_g[:, t, :], pts_planes[t][:].indirect(offsets[:]))
+            nc.vector.tensor_tensor(xc[:, t, :], pts_planes[t][:].indirect(offsets[:]), mean_g[:, t, :], ALU.subtract)
             if t == 0:
                 nc.vector.tensor_copy(scales_d[:], scales_g[:].rearrange("p (s r) -> p r s", r=PACK))
+                scale_rows = scales_d[:].rearrange("p r s -> p (r s)").bitcast(I32)
+                for j in range(1, 4):
+                    nc.scalar.dma_start(scale_rows[j:P:32, :], scale_rows[8 * j:P:32, :])
 
         xc_il = [sb.tile([P, 2 * I], BF16, name=f"xc_il{h}", align_bytes=64) for h in range(2)]
         xc_codes = [sb.tile([P, 2 * P], U32, name=f"xc_codes{h}", align_bytes=64) for h in range(2)]
         xc_scales = [sb.tile([P, 2 * P], U8, name=f"xc_scales{h}", align_bytes=64) for h in range(2)]
-        pts_dealt = pts_g[:].rearrange("p t (s r) -> p s t r", r=PACK)
-        mean_dealt = mean_g[:].rearrange("p t (s r) -> p s t r", r=PACK)
+        xc_dealt = xc[:].rearrange("p t (s r) -> p s t r", r=PACK)
         for h in range(2):
-            nc.vector.tensor_tensor(xc_il[h][:].rearrange("p (r s t) -> p s t r", r=2, t=PACK),
-                                    pts_dealt[:, :, :, 2 * h:2 * h + 2], mean_dealt[:, :, :, 2 * h:2 * h + 2],
-                                    ALU.subtract)
+            nc.vector.tensor_copy(xc_il[h][:].rearrange("p (r s t) -> p s t r", r=2, t=PACK),
+                                  xc_dealt[:, :, :, 2 * h:2 * h + 2])
 
         white_codes = sb.tile([P, K], U32, name="white_codes", align_bytes=64)
         white_scales = sb.tile([P, K], U8, name="white_scales", align_bytes=64)
@@ -131,13 +130,8 @@ def tile_attend_energyscores_pl_kernel(tc, pts, mean, white, pkpt_words, pkpt_sc
             nc.tensor.matmul_mx(a[:], lhsT=words_d[:, r, :].bitcast(FP4X4), lhsT_scale=scales_d[:, r, :],
                                 rhs=query_codes[:].bitcast(FP8X4), rhs_scale=query_scales[:],
                                 start=True, stop=True)
-            if r < PACK - 1:
-                nc.vector.scalar_tensor_tensor(y[:, r, :], neg_sharp[:, r:r + 1].to_broadcast([P, Q]),
-                                               sums[:, r:r + 1], a[:], ALU.mult, ALU.add)
-            else:
-                neg_energy = sb.tile([P, 1], F32, name=f"neg_energy{r}")
-                nc.scalar.activation(neg_energy[:], sums[:, r:r + 1], ACT.Copy, scale=neg_sharp[:, r:r + 1])
-                nc.scalar.activation(y[:, r, :], a[:], ACT.Identity, bias=neg_energy[:])
+            nc.vector.scalar_tensor_tensor(y[:, r, :], neg_sharp[:, r:r + 1].to_broadcast([P, Q]),
+                                           sums[:, r:r + 1], a[:], ALU.mult, ALU.add)
             if r % 2 == 1:
                 nc.sync.dma_start(out_rows[:, r - 1:r + 1, :], y[:, r - 1:r + 1, :])
 

from contextlib import ExitStack

import concourse.mybir as mybir

D, K, T, I, U, Q = 512, 512, 2048, 512, 256, 256
FLOPS = 2 * D * I * (K + Q)

F32 = mybir.dt.float32
BF16 = mybir.dt.bfloat16
I32 = mybir.dt.int32
U32 = mybir.dt.uint32
U16 = mybir.dt.uint16
U8 = mybir.dt.uint8
FP8X4 = mybir.dt.float8_e4m3fn_x4
FP4X4 = mybir.dt.float4_e2m1fn_x4
ALU = mybir.AluOpType
ACT = mybir.ActivationFunctionType

P = 128
PACK = 4
MEAN_WINDOW = 704
VECTOR_RUNS = 44


def tile_attend_energyscores_pl_kernel(tc, pts, mean, white, pkpt_words, pkpt_scales, query, sharp, offs, offs2,
                                        out_0, out_1, out_2):
    nc = tc.nc
    with ExitStack() as ctx:
        sb = ctx.enter_context(tc.tile_pool(name="sb", bufs=1))
        psum = ctx.enter_context(tc.psum_pool(name="psum", bufs=1))

        offsets = sb.tile([P, I // 16], U16, name="offsets")
        offsets2 = sb.tile([P, I // 16], U16, name="offsets2")
        key_scales = sb.tile([P, T], U8, name="key_scales", align_bytes=64)
        key_words = sb.tile([P, T], U16, name="key_words", align_bytes=64)
        mean_first = sb.tile([P, MEAN_WINDOW], F32, name="mean_first")
        mean_rest = sb.tile([P, 2 * U + MEAN_WINDOW], F32, name="mean_rest")
        pts_planes = [sb.tile([P, T], F32, name=f"pts_plane{t}") for t in range(PACK)]
        white_raw = [sb.tile([P, PACK, K // 2], F32, name=f"white_raw{h}") for h in range(2)]
        query_raw = sb.tile([P, PACK, Q], F32, name="query_raw")
        sharp_cols = sb.tile([P, PACK], F32, name="sharp_cols")

        nc.vector.memset(key_scales[:].bitcast(I32), 0)
        nc.vector.memset(mean_first[:, U:], 0.0)
        nc.vector.memset(mean_rest[:, 3 * U:], 0.0)

        mean_rows = mean.rearrange("(p t) u -> p (t u)", t=PACK)
        pts_rows = pts.rearrange("(p t) c -> t p c", t=PACK)
        white_rows = white.rearrange("(p t) (h k) -> h p t k", t=PACK, h=2)
        nc.sync.dma_start(offsets2[:], offs2)
        nc.sync.dma_start(mean_first[:, :U], mean_rows[:, :U])
        nc.sync.dma_start(mean_rest[:, :3 * U], mean_rows[:, U:])
        nc.sync.dma_start(offsets[:], offs)
        nc.sync.dma_start(pts_planes[0][:], pts_rows[0])
        nc.sync.dma_start(key_scales[0:P:8, :].bitcast(I32), pkpt_scales[0].bitcast(I32))
        nc.sync.dma_start(sharp_cols[:], sharp.rearrange("(p r) o -> p (r o)", r=PACK))
        for t in range(1, PACK):
            nc.sync.dma_start(pts_planes[t][:], pts_rows[t])
        for h in range(2):
            nc.sync.dma_start(white_raw[h][:], white_rows[h])
        nc.sync.dma_start(query_raw[:], query.rearrange("(p t) q -> p t q", t=PACK))
        nc.sync.dma_start(key_words[:].bitcast(I32), pkpt_words[0].bitcast(I32))

        neg_sharp = sb.tile([P, PACK], F32, name="neg_sharp")
        nc.scalar.activation(neg_sharp[:], sharp_cols[:], ACT.Copy, scale=-1.0 / K)

        mean_g = sb.tile([P, PACK, I], F32, name="mean_g")
        xc = sb.tile([P, PACK, I], F32, name="xc")
        nc.vector.tensor_copy(mean_g[:, 0, :], mean_first[:].indirect(offsets2[:]))
        for t in range(1, PACK):
            start = (t - 1) * U
            nc.vector.tensor_copy(mean_g[:, t, :], mean_rest[:, start:start + MEAN_WINDOW].indirect(offsets2[:]))
        scales_g = sb.tile([P, I], U8, name="scales_g", align_bytes=64)
        scales_d = sb.tile([P, PACK, P], U8, name="scales_d", align_bytes=64)
        nc.vector.tensor_copy(scales_g[:], key_scales[:].indirect(offsets[:]))
        for t in range(PACK):
            nc.vector.tensor_tensor(xc[:, t, :], pts_planes[t][:].indirect(offsets[:]), mean_g[:, t, :], ALU.subtract)
            if t == 0:
                nc.vector.tensor_copy(scales_d[:], scales_g[:].rearrange("p (s r) -> p r s", r=PACK))
                scale_rows = scales_d[:].rearrange("p r s -> p (r s)").bitcast(I32)
                for j in range(1, 4):
                    nc.scalar.dma_start(scale_rows[j:P:32, :], scale_rows[8 * j:P:32, :])

        xc_il = [sb.tile([P, 2 * I], BF16, name=f"xc_il{h}", align_bytes=64) for h in range(2)]
        xc_codes = [sb.tile([P, 2 * P], U32, name=f"xc_codes{h}", align_bytes=64) for h in range(2)]
        xc_scales = [sb.tile([P, 2 * P], U8, name=f"xc_scales{h}", align_bytes=64) for h in range(2)]
        xc_dealt = xc[:].rearrange("p t (s r) -> p s t r", r=PACK)
        for h in range(2):
            nc.vector.tensor_copy(xc_il[h][:].rearrange("p (r s t) -> p s t r", r=2, t=PACK),
                                  xc_dealt[:, :, :, 2 * h:2 * h + 2])

        white_codes = sb.tile([P, K], U32, name="white_codes", align_bytes=64)
        white_scales = sb.tile([P, K], U8, name="white_scales", align_bytes=64)
        for h in range(2):
            white_il = sb.tile([P, K // 2 * PACK], BF16, name=f"white_il{h}", align_bytes=64)
            nc.scalar.copy(white_il[:].rearrange("p (c i t) -> p c t i", i=4, t=PACK),
                           white_raw[h][:].rearrange("p t (c i) -> p c t i", i=4))
            cols = slice(h * K // 2, (h + 1) * K // 2)
            nc.vector.quantize_mx(white_codes[:, cols].bitcast(FP8X4), white_scales[:, cols], white_il[:])
        for h in range(2):
            nc.vector.quantize_mx(xc_codes[h][:].bitcast(FP8X4), xc_scales[h][:], xc_il[h][:])

        query_il = sb.tile([P, Q * PACK], BF16, name="query_il", align_bytes=64)
        nc.scalar.copy(query_il[:].rearrange("p (c i t) -> p c t i", i=4, t=PACK),
                       query_raw[:].rearrange("p t (c i) -> p c t i", i=4))
        query_codes = sb.tile([P, Q], U32, name="query_codes", align_bytes=64)
        query_scales = sb.tile([P, Q], U8, name="query_scales", align_bytes=64)

        words_g = sb.tile([P, I], U16, name="words_g", align_bytes=64)
        words_d = sb.tile([P, PACK, P], U16, name="words_d", align_bytes=64)
        nc.vector.tensor_copy(words_g[:], key_words[:].indirect(offsets[:]))
        nc.vector.quantize_mx(query_codes[:].bitcast(FP8X4), query_scales[:], query_il[:])
        nc.vector.tensor_copy(words_d[:], words_g[:].rearrange("p (s r) -> p r s", r=PACK))

        sums = sb.tile([P, PACK], F32, name="sums")
        squares = sb.tile([P, K], BF16, name="squares")
        for r in range(PACK):
            z = psum.tile([P, K], F32, name=f"z{r}")
            cols = slice((r % 2) * P, (r % 2 + 1) * P)
            nc.tensor.matmul_mx(z[:], lhsT=xc_codes[r // 2][:, cols].bitcast(FP8X4),
                                lhsT_scale=xc_scales[r // 2][:, cols],
                                rhs=white_codes[:].bitcast(FP8X4), rhs_scale=white_scales[:],
                                start=True, stop=True)
            nc.scalar.activation(squares[:], z[:], ACT.Square, accum_out=sums[:, r:r + 1])

        y = sb.tile([P, PACK, Q], F32, name="y")
        out_rows = out_0.rearrange("(p r) q -> p r q", r=PACK)
        for r in range(PACK):
            a = psum.tile([P, Q], F32, name=f"a{r}")
            nc.tensor.matmul_mx(a[:], lhsT=words_d[:, r, :].bitcast(FP4X4), lhsT_scale=scales_d[:, r, :],
                                rhs=query_codes[:].bitcast(FP8X4), rhs_scale=query_scales[:],
                                start=True, stop=True)
            nc.vector.scalar_tensor_tensor(y[:, r, :], neg_sharp[:, r:r + 1].to_broadcast([P, Q]),
                                           sums[:, r:r + 1], a[:], ALU.mult, ALU.add)
            if r % 2 == 1:
                nc.sync.dma_start(out_rows[:, r - 1:r + 1, :], y[:, r - 1:r + 1, :])

        y_il = sb.tile([P, Q * PACK], BF16, name="y_il", align_bytes=64)
        y_codes = sb.tile([P, Q], U32, name="y_codes", align_bytes=64)
        y_scales = sb.tile([P, Q], U8, name="y_scales", align_bytes=64)
        y_out = y_il[:].rearrange("p (c i r) -> p c r i", i=4, r=PACK)
        y_in = y[:].rearrange("p r (c i) -> p c r i", i=4)
        nc.vector.tensor_copy(y_out[:, :VECTOR_RUNS], y_in[:, :VECTOR_RUNS])
        nc.scalar.copy(y_out[:, VECTOR_RUNS:], y_in[:, VECTOR_RUNS:])
        nc.vector.quantize_mx(y_codes[:].bitcast(FP8X4), y_scales[:], y_il[:])
        nc.sync.dma_start(out_1[0].rearrange("p c r -> p (c r)").bitcast(I32), y_codes[:].bitcast(I32))
        for quad in range(4):
            queue = nc.scalar if quad % 2 == 0 else nc.sync
            queue.dma_start(out_2[0, 4 * quad:4 * quad + 4, :].bitcast(I32),
                            y_scales[32 * quad:32 * quad + 4, :].bitcast(I32))
